import numpy as np
import ml_dtypes


def mxq(x, axis, fmt="e4m3"):
    dtype, down = {"e4m3": (ml_dtypes.float8_e4m3fn, 7), "e5m2": (ml_dtypes.float8_e5m2, 14)}[fmt]
    v = np.moveaxis(np.asarray(x, np.float32).astype(ml_dtypes.bfloat16).astype(np.float64), axis, -1)
    blocks = v.reshape(v.shape[:-1] + (-1, 32))
    amax = np.abs(blocks).max(-1, keepdims=True)
    byte = np.maximum(np.where(amax > 0, np.frexp(amax)[1] - 1 + 127, 0) - down, 1)
    scale = np.exp2(byte - 127.0)
    codes = (blocks / scale).astype(np.float32).astype(dtype).astype(np.float64)
    return np.moveaxis((codes * scale).reshape(v.shape), -1, axis)


WIDE = False


def mx_kscale(k):
    if not WIDE:
        return np.ones(k)
    levels = np.array([10, -10, 5, -5, 0])
    if k % 512:
        return np.exp2(np.random.permutation(np.resize(levels, k // 32))).repeat(32)
    a = np.empty((k // 512, 16))
    for p in range(k // 512):
        a[p, :8] = np.random.permutation(np.resize(levels, 8))
        for g in range(8):
            far = levels[np.abs(levels - a[p, g]) >= 10]
            a[p, g + 8] = far[np.random.randint(len(far))]
    return np.exp2(a.ravel()).repeat(32)


BF16 = ml_dtypes.bfloat16


def bf(x):
    return np.asarray(x, np.float32).astype(BF16)


def f64(x):
    return np.asarray(x).astype(np.float64)


E2M1 = np.array([0.0, 0.5, 1.0, 1.5, 2.0, 3.0, 4.0, 6.0, -0.0, -0.5, -1.0, -1.5, -2.0, -3.0, -4.0, -6.0])


def pack_weight(w, fmt):
    k, n = w.shape
    w = f64(bf(w)).reshape(k // 32, 32, n)
    amax = np.abs(w).max(1)
    if fmt == "e4m3":
        byte = np.frexp(amax)[1] - 1 + 127 - 7
    else:
        mant, ex = np.frexp(amax / 6.0)
        byte = np.where(mant > 0.5, ex, ex - 1) + 127
    byte = np.clip(np.where(amax > 0, byte, 1), 1, 254)
    scaled = (w * np.exp2(127.0 - byte)[:, None, :]).reshape(k, n).astype(np.float32)
    by_word = np.ascontiguousarray(scaled.reshape(k // 512, 128, 4, n).transpose(0, 1, 3, 2))
    if fmt == "e4m3":
        words = by_word.astype(ml_dtypes.float8_e4m3fn).view(np.uint8)
    else:
        c = by_word.astype(ml_dtypes.float4_e2m1fn).view(np.uint8) & 0xF
        words = c[..., 0::2] | (c[..., 1::2] << 4)
    return np.ascontiguousarray(words), np.ascontiguousarray(byte.astype(np.uint8).reshape(k // 512, 16, n))


def unpack_weight(words, scales, fmt):
    g, p, n, _ = words.shape
    if fmt == "e4m3":
        vals = np.ascontiguousarray(words).view(ml_dtypes.float8_e4m3fn).astype(np.float64)
    else:
        nib = np.empty((g, p, n, 4), np.uint8)
        nib[..., 0::2] = words & 0xF
        nib[..., 1::2] = words >> 4
        vals = E2M1[nib]
    vals = vals * np.repeat(np.exp2(scales.astype(np.float64) - 127.0), 8, axis=1)[..., None]
    return vals.transpose(0, 1, 3, 2).reshape(g * 512, n)
def pack4(w):
    words, scales = pack_weight(w, "e2m1")
    return words.reshape(words.shape[0], 128, -1), scales


def unpack4(words, scales):
    return unpack_weight(words.reshape(words.shape[0], 128, -1, 2), scales, "e2m1")


T, K, F, L, N = 1024, 1024, 1536, 512, 1024


def setup_inputs():
    s, v, r = mx_kscale(K), mx_kscale(L), mx_kscale(T)
    gain_in = np.exp(0.4 * np.random.standard_normal(F))
    gain_out = np.exp(0.4 * np.random.standard_normal(N))
    w = np.random.standard_normal((K, F)) / np.sqrt(K) / T ** 0.25 * gain_in
    w_words, w_scales = pack4(w / s[:, None])
    b = np.random.standard_normal((L, N)) / np.sqrt(L) / T ** 0.25 * gain_out
    return {"x": bf(np.random.standard_normal((T, K)) * s * r[:, None]),
            "w_words": w_words,
            "w_scales": w_scales,
            "e": bf(np.random.standard_normal((T, L)) * v / r[:, None]),
            "b": bf(b / v[:, None])}


def reference(x, w_words, w_scales, e, b):
    a = np.maximum(mxq(f64(x), 1, "e4m3") @ unpack4(w_words, w_scales), 0.0)
    d = mxq(f64(e), 1, "e4m3") @ mxq(f64(b), 0, "e4m3")
    g = mxq(a, 0, "e4m3").T @ mxq(d, 0, "e4m3")
    sq = g * g
    row = sq.mean(axis=1, keepdims=True)
    col = sq.mean(axis=0, keepdims=True)
    return g / np.sqrt(row / row.mean() * col)

@@ -1,0 +1,318 @@
+from contextlib import ExitStack
+
+import concourse.mybir as mybir
+from concourse.masks import make_identity
+
+T, K, F, L, N = 1024, 1024, 1536, 512, 1024
+FLOPS = 2 * (T * K * F + T * L * N + T * F * N)
+
+F32 = mybir.dt.float32
+BF16 = mybir.dt.bfloat16
+I32 = mybir.dt.int32
+U32 = mybir.dt.uint32
+U8 = mybir.dt.uint8
+E4M3 = mybir.dt.float8_e4m3fn_x4
+E2M1 = mybir.dt.float4_e2m1fn_x4
+ACT = mybir.ActivationFunctionType
+ALU = mybir.AluOpType
+
+P = 128
+NF = F // P
+HALF = 512
+
+
+def tile_adafactor_gradient_step_s11_kernel(tc, x, w_words, w_scales, e, b, out):
+    nc = tc.nc
+    with ExitStack() as ctx:
+        keep = ctx.enter_context(tc.tile_pool(name="keep", bufs=1))
+        stage = ctx.enter_context(tc.tile_pool(name="stage", bufs=3))
+        outs = ctx.enter_context(tc.tile_pool(name="outs", bufs=8))
+        psum = ctx.enter_context(tc.psum_pool(name="psum", bufs=8))
+        ctx.enter_context(tc.manual_schedule())
+
+        ident = keep.tile([P, P], F32, name="ident")
+        ones = keep.tile([P, P], F32, name="ones")
+        dummy = keep.tile([P, 8], F32, name="dummy")
+        w_codes = keep.tile([P, 2, 2 * F], U8, name="w_codes", align_bytes=64)
+        w_scl = keep.tile([P, 2 * F], U8, name="w_scl", align_bytes=64)
+        x_raw = [keep.tile([P, 4, K], BF16, name="x_raw%d" % g, align_bytes=64) for g in range(2)]
+        e_raw = [keep.tile([P, 4, L], BF16, name="e_raw%d" % g, align_bytes=64) for g in range(2)]
+        b_raw = keep.tile([P, 4, N], BF16, name="b_raw", align_bytes=64)
+        x_grp = [[keep.tile([P, HALF * 4], BF16, name="x_grp%d%d" % (g, kp), align_bytes=64) for kp in range(2)] for g in range(2)]
+        e_grp = [keep.tile([P, HALF * 4], BF16, name="e_grp%d" % g, align_bytes=64) for g in range(2)]
+        b_grp = [keep.tile([P, HALF * 4], BF16, name="b_grp%d" % h, align_bytes=64) for h in range(2)]
+        xq = [[keep.tile([P, HALF], U32, name="xq%d%d" % (g, kp), align_bytes=64) for kp in range(2)] for g in range(2)]
+        xs = [[keep.tile([P, HALF], U8, name="xs%d%d" % (g, kp), align_bytes=64) for kp in range(2)] for g in range(2)]
+        eq = [keep.tile([P, HALF], U32, name="eq%d" % g, align_bytes=64) for g in range(2)]
+        es = [keep.tile([P, HALF], U8, name="es%d" % g, align_bytes=64) for g in range(2)]
+        bq = [keep.tile([P, HALF], U32, name="bq%d" % h, align_bytes=64) for h in range(2)]
+        bs = [keep.tile([P, HALF], U8, name="bs%d" % h, align_bytes=64) for h in range(2)]
+        aq = [[keep.tile([P, HALF], U32, name="aq%d%d" % (g, c), align_bytes=64) for c in range(3)] for g in range(2)]
+        asc = [[keep.tile([P, HALF], U8, name="as%d%d" % (g, c), align_bytes=64) for c in range(3)] for g in range(2)]
+        dq = [[keep.tile([P, HALF], U32, name="dq%d%d" % (g, h), align_bytes=64) for h in range(2)] for g in range(2)]
+        ds = [[keep.tile([P, HALF], U8, name="ds%d%d" % (g, h), align_bytes=64) for h in range(2)] for g in range(2)]
+        acc = [keep.tile([P, 2, HALF], F32, name="acc%d" % h) for h in range(2)]
+        rowsum = keep.tile([P, 2 * NF], F32, name="rowsum")
+        small = keep.tile([P, 2 * NF], F32, name="small")
+        rfac = keep.tile([P, NF], F32, name="rfac")
+        cfac = [keep.tile([P, HALF], F32, name="cfac%d" % h) for h in range(2)]
+
+        make_identity(nc, ident[:])
+        w_scl32 = w_scl[:].bitcast(I32)
+        nc.vector.memset(w_scl32, 0)
+        nc.vector.memset(ones[:], 1.0)
+        nc.scalar.activation(out=dummy[:, 0:1], in_=ones[:, 0:1], func=ACT.Abs_reciprocal_sqrt)
+
+        x_hbm = x.rearrange("(g m t) k -> g m t k", g=2, t=4)
+        e_hbm = e.rearrange("(g m t) k -> g m t k", g=2, t=4)
+        s_hbm = w_scales.bitcast(I32)
+
+        for t in range(4):
+            nc.sync.dma_start(out=x_raw[0][:, t, :], in_=x_hbm[0, :, t, :])
+        for q in range(4):
+            nc.scalar.dma_start(
+                out=w_scl32[32 * q : 32 * q + 4, :].rearrange("p (g n) -> p g n", g=2),
+                in_=s_hbm[:, 4 * q : 4 * q + 4, :].rearrange("g r n -> r g n"),
+            )
+        w_sb32 = w_codes[:].rearrange("p g c -> p (g c)").bitcast(I32).rearrange("p (g c) -> p g c", g=2)
+        w_hbm32 = w_words.bitcast(I32).rearrange("g p c -> p g c")
+        for h in range(2):
+            cols = slice(h * 384, (h + 1) * 384)
+            nc.sync.dma_start(out=w_sb32[:, :, cols], in_=w_hbm32[:, :, cols])
+        for g in range(2):
+            nc.sync.dma_start(out=e_raw[g][:], in_=e_hbm[g])
+        nc.sync.dma_start(out=b_raw[:], in_=b.rearrange("(p j) n -> p j n", j=4))
+        for h in range(2):
+            nc.sync.dma_start(out=x_raw[1][:, 2 * h : 2 * h + 2, :], in_=x_hbm[1, :, 2 * h : 2 * h + 2, :])
+
+        todo = []
+        turn = [0]
+
+        def bank():
+            return psum.tile([P, HALF], F32, name="bank")
+
+        def next_todo():
+            if todo:
+                todo.pop(0)()
+
+        def copy_out(eng, dst, src, relu=False):
+            if eng == "S":
+                if relu:
+                    nc.scalar.activation(out=dst, in_=src, func=ACT.Relu)
+                else:
+                    nc.scalar.copy(out=dst, in_=src)
+            else:
+                if relu:
+                    nc.vector.tensor_scalar_max(out=dst, in0=src, scalar1=0.0)
+                else:
+                    nc.vector.tensor_copy(out=dst, in_=src)
+                next_todo()
+
+        def pick(pattern):
+            turn[0] += 1
+            return pattern[turn[0] % len(pattern)]
+
+        def quant(codes, scl, src, a=0, z=HALF):
+            nc.vector.quantize_mx(out=codes[:, a:z].bitcast(E4M3), scales=scl[:, a:z], in_=src[:, 4 * a : 4 * z])
+
+        def turn_words(raw, kdim, kp, th, grp, eng):
+            words = raw[:].rearrange("p t k -> p (t k)").bitcast(F32)
+            ps = bank()
+            for tt in range(2):
+                for u in range(2):
+                    w0 = (2 * th + tt) * (kdim // 2) + 256 * kp
+                    c0 = u * 256 + tt * P
+                    nc.tensor.transpose(ps[:, c0 : c0 + P], words[:, w0 + u : w0 + 256 : 2], ident[:])
+            dst = grp[:].bitcast(F32)[:, th * HALF : (th + 1) * HALF]
+            copy_out(eng, dst.rearrange("p (r u) -> p r u", u=2), ps[:].rearrange("p (u r) -> p r u", u=2))
+
+        a_grp = {}
+
+        def job_a(g, fc, eng):
+            c, i = divmod(fc, 4)
+            if i == 0:
+                a_grp[g] = stage.tile([P, HALF * 4], BF16, name="a_grp", align_bytes=64)
+            grp = a_grp[g]
+            ps = bank()
+            for t in range(4):
+                for kp in range(2):
+                    nc.tensor.matmul_mx(
+                        out=ps[:, t * P : (t + 1) * P],
+                        lhsT=xq[g][kp][:, t * P : (t + 1) * P].bitcast(E4M3),
+                        lhsT_scale=xs[g][kp][:, t * P : (t + 1) * P],
+                        rhs=w_codes[:, kp, 256 * fc : 256 * (fc + 1)].bitcast(E2M1),
+                        rhs_scale=w_scl[:, kp * F + P * fc : kp * F + P * (fc + 1)],
+                        start=(kp == 0),
+                        stop=(kp == 1),
+                    )
+            copy_out(eng, grp[:, i * HALF : (i + 1) * HALF].rearrange("p (f t) -> p f t", t=4),
+                     ps[:].rearrange("p (t f) -> p f t", t=4), relu=True)
+            if i == 3:
+                todo.append(lambda: quant(aq[g][c], asc[g][c], grp))
+
+        d_grp = {}
+
+        def job_d(g, nch, eng):
+            h, i = divmod(nch, 4)
+            if i == 0:
+                d_grp[g] = stage.tile([P, HALF * 4], BF16, name="d_grp", align_bytes=64)
+            grp = d_grp[g]
+            ps = bank()
+            for t in range(4):
+                nc.tensor.matmul_mx(
+                    out=ps[:, t * P : (t + 1) * P],
+                    lhsT=eq[g][:, t * P : (t + 1) * P].bitcast(E4M3),
+                    lhsT_scale=es[g][:, t * P : (t + 1) * P],
+                    rhs=bq[h][:, i * P : (i + 1) * P].bitcast(E4M3),
+                    rhs_scale=bs[h][:, i * P : (i + 1) * P],
+                    start=True,
+                    stop=True,
+                )
+            copy_out(eng, grp[:, i * HALF : (i + 1) * HALF].rearrange("p (f t) -> p f t", t=4),
+                     ps[:].rearrange("p (t f) -> p f t", t=4))
+            if i == 3:
+                todo.append(lambda: quant(dq[g][h], ds[g][h], grp))
+
+        def gradient(f, h):
+            c, i = divmod(f, 4)
+            ps = bank()
+            for g in range(2):
+                nc.tensor.matmul_mx(
+                    out=ps[:],
+                    lhsT=aq[g][c][:, i * P : (i + 1) * P].bitcast(E4M3),
+                    lhsT_scale=asc[g][c][:, i * P : (i + 1) * P],
+                    rhs=dq[g][h][:].bitcast(E4M3),
+                    rhs_scale=ds[g][h][:],
+                    start=(g == 0),
+                    stop=(g == 1),
+                )
+            return ps
+
+        sq_pair = {}
+
+        def stats(f, h):
+            ps = gradient(f, h)
+            if f < 2:
+                sq = acc[h]
+            else:
+                if f % 2 == 0:
+                    sq_pair[h] = stage.tile([P, 2, HALF], F32, name="sq")
+                sq = sq_pair[h]
+            nc.scalar.activation(out=sq[:, f % 2, :], in_=ps[:], func=ACT.Square,
+                                 accum_out=rowsum[:, h * NF + f : h * NF + f + 1])
+            a0, a1 = acc[h][:, 0, :], acc[h][:, 1, :]
+            if 2 <= f < 8:
+                if f % 2 == 1:
+                    nc.vector.tensor_add(out=acc[h][:], in0=acc[h][:], in1=sq[:])
+                    next_todo()
+            elif f >= 8:
+                if f == 8:
+                    nc.vector.tensor_add(out=a0, in0=a0, in1=a1)
+                nc.vector.tensor_add(out=a0, in0=a0, in1=sq[:, f % 2, :])
+
+        def column_factor(h):
+            ps = bank()
+            nc.tensor.matmul(out=ps[:], lhsT=ones[:], rhs=acc[h][:, 0, :], start=True, stop=True)
+            nc.scalar.activation(out=cfac[h][:], in_=ps[:], func=ACT.Abs_reciprocal_sqrt)
+
+        for th in range(2):
+            for kp in range(2):
+                turn_words(x_raw[0], K, kp, th, x_grp[0][kp], "VS"[kp])
+            for kp in range(2):
+                quant(xq[0][kp], xs[0][kp], x_grp[0][kp], 256 * th, 256 * (th + 1))
+
+        pat = "SVS"
+        for fc in range(4):
+            job_a(0, fc, pick(pat))
+        for g in range(2):
+            for th in range(2):
+                turn_words(e_raw[g], L, 0, th, e_grp[g], pick(pat))
+            todo.append(lambda g=g: quant(eq[g], es[g], e_grp[g]))
+        for fc in range(4, 8):
+            job_a(0, fc, pick(pat))
+            i = fc - 4
+            h, v = divmod(i, 2)
+            c0 = h * HALF + v * 256
+            dst = b_grp[h][:, v * 1024 : (v + 1) * 1024].rearrange("p (c i t) -> p c t i", i=4, t=4)
+            src = b_raw[:, :, c0 : c0 + 256].rearrange("p t (c i) -> p c t i", i=4)
+            if "VSVS"[i] == "V":
+                nc.vector.tensor_copy(out=dst, in_=src)
+                next_todo()
+            elif "VSVS"[i] == "G":
+                nc.gpsimd.tensor_copy(out=dst, in_=src)
+            else:
+                nc.scalar.copy(out=dst, in_=src)
+            if v == 1:
+                todo.append(lambda h=h: quant(bq[h], bs[h], b_grp[h]))
+        for th in range(2):
+            for kp in range(2):
+                turn_words(x_raw[1], K, kp, th, x_grp[1][kp], pick(pat))
+        for kp in range(2):
+            todo.append(lambda kp=kp: quant(xq[1][kp], xs[1][kp], x_grp[1][kp]))
+
+        d_jobs = [(g, 4 * h + i) for h in range(2) for g in range(2) for i in range(4)]
+        a_jobs = [(0, fc) for fc in range(8, 12)] + [(1, fc) for fc in range(8)]
+        done_d = 0
+        pat = "SSV"
+        for i, (g, fc) in enumerate(a_jobs):
+            job_a(g, fc, pick(pat))
+            if i == 0:
+                while todo:
+                    next_todo()
+            while done_d * 3 < 4 * (i + 1):
+                job_d(*d_jobs[done_d], pick(pat))
+                done_d += 1
+        while todo:
+            next_todo()
+        job_a(1, 8, "S")
+        job_a(1, 9, "V")
+        stats(0, 0)
+        job_a(1, 10, "S")
+        stats(1, 0)
+        job_a(1, 11, "V")
+        while todo:
+            next_todo()
+        for f in range(2, 12):
+            stats(f, 0)
+        for f in range(12):
+            stats(f, 1)
+            if f == 7:
+                column_factor(0)
+
+        held = [gradient(0, 0), gradient(1, 0)]
+        nc.vector.tensor_add(out=small[:, 0:NF], in0=rowsum[:, 0:NF], in1=rowsum[:, NF : 2 * NF])
+        total_ps = bank()
+        nc.tensor.matmul(out=total_ps[:, 0 : 2 * NF], lhsT=ones[:], rhs=rowsum[:], start=True, stop=True)
+        nc.vector.reduce_sum(out=small[:, NF : NF + 1], in_=total_ps[:, 0 : 2 * NF], axis=mybir.AxisListType.X)
+        nc.vector.reciprocal(out=small[:, NF + 1 : NF + 2], in_=small[:, NF : NF + 1])
+        nc.scalar.activation(out=rfac[:], in_=small[:, 0:NF], func=ACT.Abs_reciprocal_sqrt,
+                             scale=small[:, NF + 1 : NF + 2])
+        column_factor(1)
+
+        rows = {}
+
+        def update(f, h, ps):
+            if h == 0:
+                rows[f] = outs.tile([P, N], F32, name="rows")
+            cols = slice(h * HALF, (h + 1) * HALF)
+            nc.vector.scalar_tensor_tensor(out=rows[f][:, cols], in0=ps[:], scalar=rfac[:, f : f + 1], in1=cfac[h][:],
+                                           op0=ALU.mult, op1=ALU.mult)
+
+        def store(f, cols):
+            nc.sync.dma_start(out=out[f * P : (f + 1) * P, cols], in_=rows[f][:, cols])
+
+        early = 4
+        lo, hi, full = slice(0, HALF), slice(HALF, N), slice(0, N)
+        for f in range(early):
+            update(f, 0, held[f] if f < 2 else gradient(f, 0))
+            store(f, lo)
+        for f in range(early):
+            update(f, 1, gradient(f, 1))
+            store(f, hi)
+        for f in range(early, NF):
+            for h in range(2):
+                update(f, h, gradient(f, h))
+                if f == NF - 1:
+                    store(f, (lo, hi)[h])
+            if f < NF - 1:
+                store(f, full)

@@ -27,13 +27,14 @@ def tile_adafactor_gradient_step_s11_kernel(tc, x, w_words, w_scales, e, b, out)
         keep = ctx.enter_context(tc.tile_pool(name="keep", bufs=1))
         stage = ctx.enter_context(tc.tile_pool(name="stage", bufs=3))
         outs = ctx.enter_context(tc.tile_pool(name="outs", bufs=8))
+        split = ctx.enter_context(tc.tile_pool(name="split", bufs=8))
         psum = ctx.enter_context(tc.psum_pool(name="psum", bufs=8))
         ctx.enter_context(tc.manual_schedule())
 
         ident = keep.tile([P, P], F32, name="ident")
         ones = keep.tile([P, P], F32, name="ones")
         dummy = keep.tile([P, 8], F32, name="dummy")
-        w_codes = keep.tile([P, 2, 2 * F], U8, name="w_codes", align_bytes=64)
+        w_codes = [keep.tile([P, 2, F], U8, name="w_codes%d" % h, align_bytes=64) for h in range(2)]
         w_scl = keep.tile([P, 2 * F], U8, name="w_scl", align_bytes=64)
         x_raw = [keep.tile([P, 4, K], BF16, name="x_raw%d" % g, align_bytes=64) for g in range(2)]
         e_raw = [keep.tile([P, 4, L], BF16, name="e_raw%d" % g, align_bytes=64) for g in range(2)]
@@ -57,28 +58,29 @@ def tile_adafactor_gradient_step_s11_kernel(tc, x, w_words, w_scales, e, b, out)
         rfac = keep.tile([P, NF], F32, name="rfac")
         cfac = [keep.tile([P, HALF], F32, name="cfac%d" % h) for h in range(2)]
 
+        nc.gpsimd.memset(dummy[:], 1.0)
+        nc.scalar.activation(out=dummy[:, 0:1], in_=dummy[:, 1:2], func=ACT.Abs_reciprocal_sqrt)
         make_identity(nc, ident[:])
         w_scl32 = w_scl[:].bitcast(I32)
         nc.vector.memset(w_scl32, 0)
-        nc.vector.memset(ones[:], 1.0)
-        nc.scalar.activation(out=dummy[:, 0:1], in_=ones[:, 0:1], func=ACT.Abs_reciprocal_sqrt)
 
         x_hbm = x.rearrange("(g m t) k -> g m t k", g=2, t=4)
         e_hbm = e.rearrange("(g m t) k -> g m t k", g=2, t=4)
         s_hbm = w_scales.bitcast(I32)
+        nc.vector.memset(ones[:], 1.0)
 
         for t in range(4):
             nc.sync.dma_start(out=x_raw[0][:, t, :], in_=x_hbm[0, :, t, :])
-        for q in range(4):
-            nc.scalar.dma_start(
-                out=w_scl32[32 * q : 32 * q + 4, :].rearrange("p (g n) -> p g n", g=2),
-                in_=s_hbm[:, 4 * q : 4 * q + 4, :].rearrange("g r n -> r g n"),
-            )
-        w_sb32 = w_codes[:].rearrange("p g c -> p (g c)").bitcast(I32).rearrange("p (g c) -> p g c", g=2)
+            if t == 1:
+                for q in range(4):
+                    nc.sync.dma_start(
+                        out=w_scl32[32 * q : 32 * q + 4, :].rearrange("p (g n) -> p g n", g=2),
+                        in_=s_hbm[:, 4 * q : 4 * q + 4, :].rearrange("g r n -> r g n"),
+                    )
         w_hbm32 = w_words.bitcast(I32).rearrange("g p c -> p g c")
         for h in range(2):
-            cols = slice(h * 384, (h + 1) * 384)
-            nc.sync.dma_start(out=w_sb32[:, :, cols], in_=w_hbm32[:, :, cols])
+            w_sb32 = w_codes[h][:].rearrange("p g c -> p (g c)").bitcast(I32).rearrange("p (g c) -> p g c", g=2)
+            nc.sync.dma_start(out=w_sb32, in_=w_hbm32[:, :, h * 384 : (h + 1) * 384])
         for g in range(2):
             nc.sync.dma_start(out=e_raw[g][:], in_=e_hbm[g])
         nc.sync.dma_start(out=b_raw[:], in_=b.rearrange("(p j) n -> p j n", j=4))
@@ -115,6 +117,29 @@ def tile_adafactor_gradient_step_s11_kernel(tc, x, w_words, w_scales, e, b, out)
         def quant(codes, scl, src, a=0, z=HALF):
             nc.vector.quantize_mx(out=codes[:, a:z].bitcast(E4M3), scales=scl[:, a:z], in_=src[:, 4 * a : 4 * z])
 
+        def split_words(raw, kdim, t, eng):
+            n = kdim // 2
+            dst = split.tile([P, n], F32, name="split%d" % kdim)
+            d = dst[:].rearrange("p (k u q) -> p k u q", u=2, q=P)
+            s = raw[:, t, :].bitcast(F32).rearrange("p (k q u) -> p k u q", u=2, q=P)
+            if eng == "G":
+                nc.gpsimd.tensor_copy(out=d.bitcast(I32), in_=s.bitcast(I32))
+            elif eng == "S":
+                nc.scalar.copy(out=d, in_=s)
+            else:
+                nc.vector.tensor_copy(out=d, in_=s)
+            return dst
+
+        def turn_split(tiles, kp, th, grp, eng):
+            ps = bank()
+            for tt in range(2):
+                for u in range(2):
+                    w0 = 256 * kp + P * u
+                    c0 = u * 256 + tt * P
+                    nc.tensor.transpose(ps[:, c0 : c0 + P], tiles[2 * th + tt][:, w0 : w0 + P], ident[:])
+            dst = grp[:].bitcast(F32)[:, th * HALF : (th + 1) * HALF]
+            copy_out(eng, dst.rearrange("p (r u) -> p r u", u=2), ps[:].rearrange("p (u r) -> p r u", u=2))
+
         def turn_words(raw, kdim, kp, th, grp, eng):
             words = raw[:].rearrange("p t k -> p (t k)").bitcast(F32)
             ps = bank()
@@ -128,27 +153,33 @@ def tile_adafactor_gradient_step_s11_kernel(tc, x, w_words, w_scales, e, b, out)
 
         a_grp = {}
 
-        def job_a(g, fc, eng):
-            c, i = divmod(fc, 4)
-            if i == 0:
-                a_grp[g] = stage.tile([P, HALF * 4], BF16, name="a_grp", align_bytes=64)
-            grp = a_grp[g]
-            ps = bank()
-            for t in range(4):
+        def a_products(ps, g, fc, ts):
+            for t in ts:
                 for kp in range(2):
                     nc.tensor.matmul_mx(
                         out=ps[:, t * P : (t + 1) * P],
                         lhsT=xq[g][kp][:, t * P : (t + 1) * P].bitcast(E4M3),
                         lhsT_scale=xs[g][kp][:, t * P : (t + 1) * P],
-                        rhs=w_codes[:, kp, 256 * fc : 256 * (fc + 1)].bitcast(E2M1),
+                        rhs=w_codes[fc // 6][:, kp, 256 * (fc % 6) : 256 * (fc % 6 + 1)].bitcast(E2M1),
                         rhs_scale=w_scl[:, kp * F + P * fc : kp * F + P * (fc + 1)],
                         start=(kp == 0),
                         stop=(kp == 1),
                     )
+
+        def a_out(ps, g, fc, eng):
+            c, i = divmod(fc, 4)
+            if i == 0:
+                a_grp[g] = stage.tile([P, HALF * 4], BF16, name="a_grp", align_bytes=64)
+            grp = a_grp[g]
             copy_out(eng, grp[:, i * HALF : (i + 1) * HALF].rearrange("p (f t) -> p f t", t=4),
                      ps[:].rearrange("p (t f) -> p f t", t=4), relu=True)
             if i == 3:
                 todo.append(lambda: quant(aq[g][c], asc[g][c], grp))
+
+        def job_a(g, fc, eng):
+            ps = bank()
+            a_products(ps, g, fc, range(4))
+            a_out(ps, g, fc, eng)
 
         d_grp = {}
 
@@ -201,18 +232,19 @@ def tile_adafactor_gradient_step_s11_kernel(tc, x, w_words, w_scales, e, b, out)
             nc.scalar.activation(out=sq[:, f % 2, :], in_=ps[:], func=ACT.Square,
                                  accum_out=rowsum[:, h * NF + f : h * NF + f + 1])
             a0, a1 = acc[h][:, 0, :], acc[h][:, 1, :]
-            if 2 <= f < 8:
-                if f % 2 == 1:
-                    nc.vector.tensor_add(out=acc[h][:], in0=acc[h][:], in1=sq[:])
-                    next_todo()
-            elif f >= 8:
-                if f == 8:
-                    nc.vector.tensor_add(out=a0, in0=a0, in1=a1)
+            pairs = NF if h == 0 else NF - 4
+            if f % 2 == 1 and 2 <= f < pairs:
+                nc.vector.tensor_add(out=acc[h][:], in0=acc[h][:], in1=sq[:])
+                next_todo()
+            if f == pairs - 1:
+                nc.vector.tensor_add(out=a0, in0=a0, in1=a1)
+            if pairs <= f < NF - 1:
                 nc.vector.tensor_add(out=a0, in0=a0, in1=sq[:, f % 2, :])
 
-        def column_factor(h):
-            ps = bank()
-            nc.tensor.matmul(out=ps[:], lhsT=ones[:], rhs=acc[h][:, 0, :], start=True, stop=True)
+        def column_sum(ps, part, start, stop):
+            nc.tensor.matmul(out=ps[:], lhsT=ones[:], rhs=part, start=start, stop=stop)
+
+        def column_factor(h, ps):
             nc.scalar.activation(out=cfac[h][:], in_=ps[:], func=ACT.Abs_reciprocal_sqrt)
 
         for th in range(2):
@@ -222,8 +254,12 @@ def tile_adafactor_gradient_step_s11_kernel(tc, x, w_words, w_scales, e, b, out)
                 quant(xq[0][kp], xs[0][kp], x_grp[0][kp], 256 * th, 256 * (th + 1))
 
         pat = "SVS"
+        first = [bank() for fc in range(4)]
+        for ts in ((0, 1), (2, 3)):
+            for fc in range(4):
+                a_products(first[fc], 0, fc, ts)
         for fc in range(4):
-            job_a(0, fc, pick(pat))
+            a_out(first[fc], 0, fc, pick(pat))
         for g in range(2):
             for th in range(2):
                 turn_words(e_raw[g], L, 0, th, e_grp[g], pick(pat))
@@ -264,30 +300,38 @@ def tile_adafactor_gradient_step_s11_kernel(tc, x, w_words, w_scales, e, b, out)
                 done_d += 1
         while todo:
             next_todo()
-        job_a(1, 8, "S")
-        job_a(1, 9, "V")
+        job_a(1, 8, "V")
         stats(0, 0)
-        job_a(1, 10, "S")
+        job_a(1, 9, "V")
         stats(1, 0)
+        job_a(1, 10, "V")
+        stats(2, 0)
         job_a(1, 11, "V")
+        stats(3, 0)
         while todo:
             next_todo()
-        for f in range(2, 12):
+        for f in range(4, 12):
             stats(f, 0)
         for f in range(12):
             stats(f, 1)
-            if f == 7:
-                column_factor(0)
 
-        held = [gradient(0, 0), gradient(1, 0)]
-        nc.vector.tensor_add(out=small[:, 0:NF], in0=rowsum[:, 0:NF], in1=rowsum[:, NF : 2 * NF])
+        col0_ps = bank()
+        column_sum(col0_ps, acc[0][:, 0, :], True, True)
+        column_factor(0, col0_ps)
         total_ps = bank()
         nc.tensor.matmul(out=total_ps[:, 0 : 2 * NF], lhsT=ones[:], rhs=rowsum[:], start=True, stop=True)
+        held = [gradient(0, 0), gradient(1, 0)]
+        nc.vector.tensor_add(out=small[:, 0:NF], in0=rowsum[:, 0:NF], in1=rowsum[:, NF : 2 * NF])
         nc.vector.reduce_sum(out=small[:, NF : NF + 1], in_=total_ps[:, 0 : 2 * NF], axis=mybir.AxisListType.X)
         nc.vector.reciprocal(out=small[:, NF + 1 : NF + 2], in_=small[:, NF : NF + 1])
         nc.scalar.activation(out=rfac[:], in_=small[:, 0:NF], func=ACT.Abs_reciprocal_sqrt,
                              scale=small[:, NF + 1 : NF + 2])
-        column_factor(1)
+        col_ps = bank()
+        held.append(gradient(2, 0))
+        column_sum(col_ps, acc[1][:, 0, :], True, False)
+        held.append(gradient(3, 0))
+        column_sum(col_ps, sq_pair[1][:, 1, :], False, True)
+        column_factor(1, col_ps)
 
         rows = {}
 
@@ -301,10 +345,10 @@ def tile_adafactor_gradient_step_s11_kernel(tc, x, w_words, w_scales, e, b, out)
         def store(f, cols):
             nc.sync.dma_start(out=out[f * P : (f + 1) * P, cols], in_=rows[f][:, cols])
 
-        early = 4
+        early = 5
         lo, hi, full = slice(0, HALF), slice(HALF, N), slice(0, N)
         for f in range(early):
-            update(f, 0, held[f] if f < 2 else gradient(f, 0))
+            update(f, 0, held[f] if f < len(held) else gradient(f, 0))
             store(f, lo)
         for f in range(early):
             update(f, 1, gradient(f, 1))

@@ -26,7 +26,7 @@ def tile_adafactor_gradient_step_s11_kernel(tc, x, w_words, w_scales, e, b, out)
     with ExitStack() as ctx:
         keep = ctx.enter_context(tc.tile_pool(name="keep", bufs=1))
         stage = ctx.enter_context(tc.tile_pool(name="stage", bufs=3))
-        outs = ctx.enter_context(tc.tile_pool(name="outs", bufs=8))
+        outs = ctx.enter_context(tc.tile_pool(name="outs", bufs=12))
         split = ctx.enter_context(tc.tile_pool(name="split", bufs=8))
         psum = ctx.enter_context(tc.psum_pool(name="psum", bufs=8))
         ctx.enter_context(tc.manual_schedule())
@@ -58,11 +58,20 @@ def tile_adafactor_gradient_step_s11_kernel(tc, x, w_words, w_scales, e, b, out)
         rfac = keep.tile([P, NF], F32, name="rfac")
         cfac = [keep.tile([P, HALF], F32, name="cfac%d" % h) for h in range(2)]
 
+        def bank():
+            return psum.tile([P, HALF], F32, name="bank")
+
         nc.gpsimd.memset(dummy[:], 1.0)
         nc.scalar.activation(out=dummy[:, 0:1], in_=dummy[:, 1:2], func=ACT.Abs_reciprocal_sqrt)
         make_identity(nc, ident[:])
         w_scl32 = w_scl[:].bitcast(I32)
+
+        warm = keep.tile([P, HALF], BF16, name="warm")
+        nc.vector.memset(warm[:], 0.0)
         nc.vector.memset(w_scl32, 0)
+        warm_ps = bank()
+        for i in range(4):
+            nc.tensor.matmul(out=warm_ps[:], lhsT=warm[:, 0:P], rhs=warm[:], start=True, stop=True)
 
         x_hbm = x.rearrange("(g m t) k -> g m t k", g=2, t=4)
         e_hbm = e.rearrange("(g m t) k -> g m t k", g=2, t=4)
@@ -89,9 +98,6 @@ def tile_adafactor_gradient_step_s11_kernel(tc, x, w_words, w_scales, e, b, out)
 
         todo = []
         turn = [0]
-
-        def bank():
-            return psum.tile([P, HALF], F32, name="bank")
 
         def next_todo():
             if todo:
@@ -219,27 +225,19 @@ def tile_adafactor_gradient_step_s11_kernel(tc, x, w_words, w_scales, e, b, out)
                 )
             return ps
 
-        sq_pair = {}
-
         def stats(f, h):
             ps = gradient(f, h)
-            if f < 2:
-                sq = acc[h]
-            else:
-                if f % 2 == 0:
-                    sq_pair[h] = stage.tile([P, 2, HALF], F32, name="sq")
-                sq = sq_pair[h]
-            nc.scalar.activation(out=sq[:, f % 2, :], in_=ps[:], func=ACT.Square,
+            lane = acc[h][:, f % 2, :]
+            sq = lane
+            if f >= 2:
+                sq_tile = stage.tile([P, HALF], F32, name="sq", bufs=4)
+                sq = sq_tile[:]
+            nc.scalar.activation(out=sq, in_=ps[:], func=ACT.Square,
                                  accum_out=rowsum[:, h * NF + f : h * NF + f + 1])
-            a0, a1 = acc[h][:, 0, :], acc[h][:, 1, :]
-            pairs = NF if h == 0 else NF - 4
-            if f % 2 == 1 and 2 <= f < pairs:
-                nc.vector.tensor_add(out=acc[h][:], in0=acc[h][:], in1=sq[:])
+            if f >= 2 and (f, h) != (NF - 1, 1):
+                nc.vector.tensor_add(out=lane, in0=lane, in1=sq)
                 next_todo()
-            if f == pairs - 1:
-                nc.vector.tensor_add(out=a0, in0=a0, in1=a1)
-            if pairs <= f < NF - 1:
-                nc.vector.tensor_add(out=a0, in0=a0, in1=sq[:, f % 2, :])
+            return sq
 
         def column_sum(ps, part, start, stop):
             nc.tensor.matmul(out=ps[:], lhsT=ones[:], rhs=part, start=start, stop=stop)
@@ -252,6 +250,9 @@ def tile_adafactor_gradient_step_s11_kernel(tc, x, w_words, w_scales, e, b, out)
                 turn_words(x_raw[0], K, kp, th, x_grp[0][kp], "VS"[kp])
             for kp in range(2):
                 quant(xq[0][kp], xs[0][kp], x_grp[0][kp], 256 * th, 256 * (th + 1))
+            if th == 0:
+                for i in range(2):
+                    nc.tensor.matmul(out=warm_ps[:], lhsT=warm[:, 0:P], rhs=warm[:], start=True, stop=True)
 
         pat = "SVS"
         first = [bank() for fc in range(4)]
@@ -313,50 +314,49 @@ def tile_adafactor_gradient_step_s11_kernel(tc, x, w_words, w_scales, e, b, out)
         for f in range(4, 12):
             stats(f, 0)
         for f in range(12):
-            stats(f, 1)
+            last = stats(f, 1)
+            if f == 2:
+                nc.vector.tensor_add(out=acc[0][:, 0, :], in0=acc[0][:, 0, :], in1=acc[0][:, 1, :])
 
-        col0_ps = bank()
-        column_sum(col0_ps, acc[0][:, 0, :], True, True)
-        column_factor(0, col0_ps)
+        col_ps = bank()
+        column_sum(col_ps, acc[0][:, 0, :], True, True)
+        column_factor(0, col_ps)
         total_ps = bank()
         nc.tensor.matmul(out=total_ps[:, 0 : 2 * NF], lhsT=ones[:], rhs=rowsum[:], start=True, stop=True)
-        held = [gradient(0, 0), gradient(1, 0)]
+        held = [gradient(f, 0) for f in range(2)]
         nc.vector.tensor_add(out=small[:, 0:NF], in0=rowsum[:, 0:NF], in1=rowsum[:, NF : 2 * NF])
         nc.vector.reduce_sum(out=small[:, NF : NF + 1], in_=total_ps[:, 0 : 2 * NF], axis=mybir.AxisListType.X)
         nc.vector.reciprocal(out=small[:, NF + 1 : NF + 2], in_=small[:, NF : NF + 1])
+        nc.vector.tensor_add(out=acc[1][:, 1, :], in0=acc[1][:, 1, :], in1=last)
         nc.scalar.activation(out=rfac[:], in_=small[:, 0:NF], func=ACT.Abs_reciprocal_sqrt,
                              scale=small[:, NF + 1 : NF + 2])
+
         col_ps = bank()
-        held.append(gradient(2, 0))
         column_sum(col_ps, acc[1][:, 0, :], True, False)
-        held.append(gradient(3, 0))
-        column_sum(col_ps, sq_pair[1][:, 1, :], False, True)
+        held.append(gradient(2, 0))
+        column_sum(col_ps, acc[1][:, 1, :], False, True)
         column_factor(1, col_ps)
 
         rows = {}
 
         def update(f, h, ps):
             if h == 0:
-                rows[f] = outs.tile([P, N], F32, name="rows")
-            cols = slice(h * HALF, (h + 1) * HALF)
-            nc.vector.scalar_tensor_tensor(out=rows[f][:, cols], in0=ps[:], scalar=rfac[:, f : f + 1], in1=cfac[h][:],
-                                           op0=ALU.mult, op1=ALU.mult)
+                rows[f] = outs.tile([P, N], F32, name="row")
+            nc.vector.scalar_tensor_tensor(out=rows[f][:, h * HALF : (h + 1) * HALF], in0=ps[:], scalar=rfac[:, f : f + 1],
+                                           in1=cfac[h][:], op0=ALU.mult, op1=ALU.mult)
 
         def store(f, cols):
             nc.sync.dma_start(out=out[f * P : (f + 1) * P, cols], in_=rows[f][:, cols])
 
-        early = 5
-        lo, hi, full = slice(0, HALF), slice(HALF, N), slice(0, N)
-        for f in range(early):
-            update(f, 0, held[f] if f < len(held) else gradient(f, 0))
-            store(f, lo)
-        for f in range(early):
-            update(f, 1, gradient(f, 1))
-            store(f, hi)
-        for f in range(early, NF):
+        halves = (slice(0, HALF), slice(HALF, N))
+        for h in range(2):
+            for f in range(4):
+                update(f, h, held[f] if h == 0 and f < len(held) else gradient(f, h))
+                store(f, halves[h])
+        for f in range(4, NF):
             for h in range(2):
                 update(f, h, gradient(f, h))
                 if f == NF - 1:
-                    store(f, (lo, hi)[h])
+                    store(f, halves[h])
             if f < NF - 1:
-                store(f, full)
+                store(f, slice(0, N))

from contextlib import ExitStack

import concourse.mybir as mybir
from concourse.masks import make_identity

T, K, F, L, N = 1024, 1024, 1536, 512, 1024
FLOPS = 2 * (T * K * F + T * L * N + T * F * N)

F32 = mybir.dt.float32
BF16 = mybir.dt.bfloat16
I32 = mybir.dt.int32
U32 = mybir.dt.uint32
U8 = mybir.dt.uint8
E4M3 = mybir.dt.float8_e4m3fn_x4
E2M1 = mybir.dt.float4_e2m1fn_x4
ACT = mybir.ActivationFunctionType
ALU = mybir.AluOpType

P = 128
NF = F // P
HALF = 512


def tile_adafactor_gradient_step_s11_kernel(tc, x, w_words, w_scales, e, b, out):
    nc = tc.nc
    with ExitStack() as ctx:
        keep = ctx.enter_context(tc.tile_pool(name="keep", bufs=1))
        stage = ctx.enter_context(tc.tile_pool(name="stage", bufs=3))
        outs = ctx.enter_context(tc.tile_pool(name="outs", bufs=12))
        split = ctx.enter_context(tc.tile_pool(name="split", bufs=8))
        psum = ctx.enter_context(tc.psum_pool(name="psum", bufs=8))
        ctx.enter_context(tc.manual_schedule())

        ident = keep.tile([P, P], F32, name="ident")
        ones = keep.tile([P, P], F32, name="ones")
        dummy = keep.tile([P, 8], F32, name="dummy")
        w_codes = [keep.tile([P, 2, F], U8, name="w_codes%d" % h, align_bytes=64) for h in range(2)]
        w_scl = keep.tile([P, 2 * F], U8, name="w_scl", align_bytes=64)
        x_raw = [keep.tile([P, 4, K], BF16, name="x_raw%d" % g, align_bytes=64) for g in range(2)]
        e_raw = [keep.tile([P, 4, L], BF16, name="e_raw%d" % g, align_bytes=64) for g in range(2)]
        b_raw = keep.tile([P, 4, N], BF16, name="b_raw", align_bytes=64)
        x_grp = [[keep.tile([P, HALF * 4], BF16, name="x_grp%d%d" % (g, kp), align_bytes=64) for kp in range(2)] for g in range(2)]
        e_grp = [keep.tile([P, HALF * 4], BF16, name="e_grp%d" % g, align_bytes=64) for g in range(2)]
        b_grp = [keep.tile([P, HALF * 4], BF16, name="b_grp%d" % h, align_bytes=64) for h in range(2)]
        xq = [[keep.tile([P, HALF], U32, name="xq%d%d" % (g, kp), align_bytes=64) for kp in range(2)] for g in range(2)]
        xs = [[keep.tile([P, HALF], U8, name="xs%d%d" % (g, kp), align_bytes=64) for kp in range(2)] for g in range(2)]
        eq = [keep.tile([P, HALF], U32, name="eq%d" % g, align_bytes=64) for g in range(2)]
        es = [keep.tile([P, HALF], U8, name="es%d" % g, align_bytes=64) for g in range(2)]
        bq = [keep.tile([P, HALF], U32, name="bq%d" % h, align_bytes=64) for h in range(2)]
        bs = [keep.tile([P, HALF], U8, name="bs%d" % h, align_bytes=64) for h in range(2)]
        aq = [[keep.tile([P, HALF], U32, name="aq%d%d" % (g, c), align_bytes=64) for c in range(3)] for g in range(2)]
        asc = [[keep.tile([P, HALF], U8, name="as%d%d" % (g, c), align_bytes=64) for c in range(3)] for g in range(2)]
        dq = [[keep.tile([P, HALF], U32, name="dq%d%d" % (g, h), align_bytes=64) for h in range(2)] for g in range(2)]
        ds = [[keep.tile([P, HALF], U8, name="ds%d%d" % (g, h), align_bytes=64) for h in range(2)] for g in range(2)]
        acc = [keep.tile([P, 2, HALF], F32, name="acc%d" % h) for h in range(2)]
        rowsum = keep.tile([P, 2 * NF], F32, name="rowsum")
        small = keep.tile([P, 2 * NF], F32, name="small")
        rfac = keep.tile([P, NF], F32, name="rfac")
        cfac = [keep.tile([P, HALF], F32, name="cfac%d" % h) for h in range(2)]

        def bank():
            return psum.tile([P, HALF], F32, name="bank")

        nc.gpsimd.memset(dummy[:], 1.0)
        nc.scalar.activation(out=dummy[:, 0:1], in_=dummy[:, 1:2], func=ACT.Abs_reciprocal_sqrt)
        make_identity(nc, ident[:])
        w_scl32 = w_scl[:].bitcast(I32)

        warm = keep.tile([P, HALF], BF16, name="warm")
        nc.vector.memset(warm[:], 0.0)
        nc.vector.memset(w_scl32, 0)
        warm_ps = bank()
        for i in range(4):
            nc.tensor.matmul(out=warm_ps[:], lhsT=warm[:, 0:P], rhs=warm[:], start=True, stop=True)

        x_hbm = x.rearrange("(g m t) k -> g m t k", g=2, t=4)
        e_hbm = e.rearrange("(g m t) k -> g m t k", g=2, t=4)
        s_hbm = w_scales.bitcast(I32)
        nc.vector.memset(ones[:], 1.0)

        for t in range(4):
            nc.sync.dma_start(out=x_raw[0][:, t, :], in_=x_hbm[0, :, t, :])
            if t == 1:
                for q in range(4):
                    nc.sync.dma_start(
                        out=w_scl32[32 * q : 32 * q + 4, :].rearrange("p (g n) -> p g n", g=2),
                        in_=s_hbm[:, 4 * q : 4 * q + 4, :].rearrange("g r n -> r g n"),
                    )
        w_hbm32 = w_words.bitcast(I32).rearrange("g p c -> p g c")
        for h in range(2):
            w_sb32 = w_codes[h][:].rearrange("p g c -> p (g c)").bitcast(I32).rearrange("p (g c) -> p g c", g=2)
            nc.sync.dma_start(out=w_sb32, in_=w_hbm32[:, :, h * 384 : (h + 1) * 384])
        for g in range(2):
            nc.sync.dma_start(out=e_raw[g][:], in_=e_hbm[g])
        nc.sync.dma_start(out=b_raw[:], in_=b.rearrange("(p j) n -> p j n", j=4))
        for h in range(2):
            nc.sync.dma_start(out=x_raw[1][:, 2 * h : 2 * h + 2, :], in_=x_hbm[1, :, 2 * h : 2 * h + 2, :])

        todo = []
        turn = [0]

        def next_todo():
            if todo:
                todo.pop(0)()

        def copy_out(eng, dst, src, relu=False):
            if eng == "S":
                if relu:
                    nc.scalar.activation(out=dst, in_=src, func=ACT.Relu)
                else:
                    nc.scalar.copy(out=dst, in_=src)
            else:
                if relu:
                    nc.vector.tensor_scalar_max(out=dst, in0=src, scalar1=0.0)
                else:
                    nc.vector.tensor_copy(out=dst, in_=src)
                next_todo()

        def pick(pattern):
            turn[0] += 1
            return pattern[turn[0] % len(pattern)]

        def quant(codes, scl, src, a=0, z=HALF):
            nc.vector.quantize_mx(out=codes[:, a:z].bitcast(E4M3), scales=scl[:, a:z], in_=src[:, 4 * a : 4 * z])

        def split_words(raw, kdim, t, eng):
            n = kdim // 2
            dst = split.tile([P, n], F32, name="split%d" % kdim)
            d = dst[:].rearrange("p (k u q) -> p k u q", u=2, q=P)
            s = raw[:, t, :].bitcast(F32).rearrange("p (k q u) -> p k u q", u=2, q=P)
            if eng == "G":
                nc.gpsimd.tensor_copy(out=d.bitcast(I32), in_=s.bitcast(I32))
            elif eng == "S":
                nc.scalar.copy(out=d, in_=s)
            else:
                nc.vector.tensor_copy(out=d, in_=s)
            return dst

        def turn_split(tiles, kp, th, grp, eng):
            ps = bank()
            for tt in range(2):
                for u in range(2):
                    w0 = 256 * kp + P * u
                    c0 = u * 256 + tt * P
                    nc.tensor.transpose(ps[:, c0 : c0 + P], tiles[2 * th + tt][:, w0 : w0 + P], ident[:])
            dst = grp[:].bitcast(F32)[:, th * HALF : (th + 1) * HALF]
            copy_out(eng, dst.rearrange("p (r u) -> p r u", u=2), ps[:].rearrange("p (u r) -> p r u", u=2))

        def turn_words(raw, kdim, kp, th, grp, eng):
            words = raw[:].rearrange("p t k -> p (t k)").bitcast(F32)
            ps = bank()
            for tt in range(2):
                for u in range(2):
                    w0 = (2 * th + tt) * (kdim // 2) + 256 * kp
                    c0 = u * 256 + tt * P
                    nc.tensor.transpose(ps[:, c0 : c0 + P], words[:, w0 + u : w0 + 256 : 2], ident[:])
            dst = grp[:].bitcast(F32)[:, th * HALF : (th + 1) * HALF]
            copy_out(eng, dst.rearrange("p (r u) -> p r u", u=2), ps[:].rearrange("p (u r) -> p r u", u=2))

        a_grp = {}

        def a_products(ps, g, fc, ts):
            for t in ts:
                for kp in range(2):
                    nc.tensor.matmul_mx(
                        out=ps[:, t * P : (t + 1) * P],
                        lhsT=xq[g][kp][:, t * P : (t + 1) * P].bitcast(E4M3),
                        lhsT_scale=xs[g][kp][:, t * P : (t + 1) * P],
                        rhs=w_codes[fc // 6][:, kp, 256 * (fc % 6) : 256 * (fc % 6 + 1)].bitcast(E2M1),
                        rhs_scale=w_scl[:, kp * F + P * fc : kp * F + P * (fc + 1)],
                        start=(kp == 0),
                        stop=(kp == 1),
                    )

        def a_out(ps, g, fc, eng):
            c, i = divmod(fc, 4)
            if i == 0:
                a_grp[g] = stage.tile([P, HALF * 4], BF16, name="a_grp", align_bytes=64)
            grp = a_grp[g]
            copy_out(eng, grp[:, i * HALF : (i + 1) * HALF].rearrange("p (f t) -> p f t", t=4),
                     ps[:].rearrange("p (t f) -> p f t", t=4), relu=True)
            if i == 3:
                todo.append(lambda: quant(aq[g][c], asc[g][c], grp))

        def job_a(g, fc, eng):
            ps = bank()
            a_products(ps, g, fc, range(4))
            a_out(ps, g, fc, eng)

        d_grp = {}

        def job_d(g, nch, eng):
            h, i = divmod(nch, 4)
            if i == 0:
                d_grp[g] = stage.tile([P, HALF * 4], BF16, name="d_grp", align_bytes=64)
            grp = d_grp[g]
            ps = bank()
            for t in range(4):
                nc.tensor.matmul_mx(
                    out=ps[:, t * P : (t + 1) * P],
                    lhsT=eq[g][:, t * P : (t + 1) * P].bitcast(E4M3),
                    lhsT_scale=es[g][:, t * P : (t + 1) * P],
                    rhs=bq[h][:, i * P : (i + 1) * P].bitcast(E4M3),
                    rhs_scale=bs[h][:, i * P : (i + 1) * P],
                    start=True,
                    stop=True,
                )
            copy_out(eng, grp[:, i * HALF : (i + 1) * HALF].rearrange("p (f t) -> p f t", t=4),
                     ps[:].rearrange("p (t f) -> p f t", t=4))
            if i == 3:
                todo.append(lambda: quant(dq[g][h], ds[g][h], grp))

        def gradient(f, h):
            c, i = divmod(f, 4)
            ps = bank()
            for g in range(2):
                nc.tensor.matmul_mx(
                    out=ps[:],
                    lhsT=aq[g][c][:, i * P : (i + 1) * P].bitcast(E4M3),
                    lhsT_scale=asc[g][c][:, i * P : (i + 1) * P],
                    rhs=dq[g][h][:].bitcast(E4M3),
                    rhs_scale=ds[g][h][:],
                    start=(g == 0),
                    stop=(g == 1),
                )
            return ps

        def stats(f, h):
            ps = gradient(f, h)
            lane = acc[h][:, f % 2, :]
            sq = lane
            if f >= 2:
                sq_tile = stage.tile([P, HALF], F32, name="sq", bufs=4)
                sq = sq_tile[:]
            nc.scalar.activation(out=sq, in_=ps[:], func=ACT.Square,
                                 accum_out=rowsum[:, h * NF + f : h * NF + f + 1])
            if f >= 2 and (f, h) != (NF - 1, 1):
                nc.vector.tensor_add(out=lane, in0=lane, in1=sq)
                next_todo()
            return sq

        def column_sum(ps, part, start, stop):
            nc.tensor.matmul(out=ps[:], lhsT=ones[:], rhs=part, start=start, stop=stop)

        def column_factor(h, ps):
            nc.scalar.activation(out=cfac[h][:], in_=ps[:], func=ACT.Abs_reciprocal_sqrt)

        for th in range(2):
            for kp in range(2):
                turn_words(x_raw[0], K, kp, th, x_grp[0][kp], "VS"[kp])
            for kp in range(2):
                quant(xq[0][kp], xs[0][kp], x_grp[0][kp], 256 * th, 256 * (th + 1))
            if th == 0:
                for i in range(2):
                    nc.tensor.matmul(out=warm_ps[:], lhsT=warm[:, 0:P], rhs=warm[:], start=True, stop=True)

        pat = "SVS"
        first = [bank() for fc in range(4)]
        for ts in ((0, 1), (2, 3)):
            for fc in range(4):
                a_products(first[fc], 0, fc, ts)
        for fc in range(4):
            a_out(first[fc], 0, fc, pick(pat))
        for g in range(2):
            for th in range(2):
                turn_words(e_raw[g], L, 0, th, e_grp[g], pick(pat))
            todo.append(lambda g=g: quant(eq[g], es[g], e_grp[g]))
        for fc in range(4, 8):
            job_a(0, fc, pick(pat))
            i = fc - 4
            h, v = divmod(i, 2)
            c0 = h * HALF + v * 256
            dst = b_grp[h][:, v * 1024 : (v + 1) * 1024].rearrange("p (c i t) -> p c t i", i=4, t=4)
            src = b_raw[:, :, c0 : c0 + 256].rearrange("p t (c i) -> p c t i", i=4)
            if "VSVS"[i] == "V":
                nc.vector.tensor_copy(out=dst, in_=src)
                next_todo()
            elif "VSVS"[i] == "G":
                nc.gpsimd.tensor_copy(out=dst, in_=src)
            else:
                nc.scalar.copy(out=dst, in_=src)
            if v == 1:
                todo.append(lambda h=h: quant(bq[h], bs[h], b_grp[h]))
        for th in range(2):
            for kp in range(2):
                turn_words(x_raw[1], K, kp, th, x_grp[1][kp], pick(pat))
        for kp in range(2):
            todo.append(lambda kp=kp: quant(xq[1][kp], xs[1][kp], x_grp[1][kp]))

        d_jobs = [(g, 4 * h + i) for h in range(2) for g in range(2) for i in range(4)]
        a_jobs = [(0, fc) for fc in range(8, 12)] + [(1, fc) for fc in range(8)]
        done_d = 0
        pat = "SSV"
        for i, (g, fc) in enumerate(a_jobs):
            job_a(g, fc, pick(pat))
            if i == 0:
                while todo:
                    next_todo()
            while done_d * 3 < 4 * (i + 1):
                job_d(*d_jobs[done_d], pick(pat))
                done_d += 1
        while todo:
            next_todo()
        job_a(1, 8, "V")
        stats(0, 0)
        job_a(1, 9, "V")
        stats(1, 0)
        job_a(1, 10, "V")
        stats(2, 0)
        job_a(1, 11, "V")
        stats(3, 0)
        while todo:
            next_todo()
        for f in range(4, 12):
            stats(f, 0)
        for f in range(12):
            last = stats(f, 1)
            if f == 2:
                nc.vector.tensor_add(out=acc[0][:, 0, :], in0=acc[0][:, 0, :], in1=acc[0][:, 1, :])

        col_ps = bank()
        column_sum(col_ps, acc[0][:, 0, :], True, True)
        column_factor(0, col_ps)
        total_ps = bank()
        nc.tensor.matmul(out=total_ps[:, 0 : 2 * NF], lhsT=ones[:], rhs=rowsum[:], start=True, stop=True)
        held = [gradient(f, 0) for f in range(2)]
        nc.vector.tensor_add(out=small[:, 0:NF], in0=rowsum[:, 0:NF], in1=rowsum[:, NF : 2 * NF])
        nc.vector.reduce_sum(out=small[:, NF : NF + 1], in_=total_ps[:, 0 : 2 * NF], axis=mybir.AxisListType.X)
        nc.vector.reciprocal(out=small[:, NF + 1 : NF + 2], in_=small[:, NF : NF + 1])
        nc.vector.tensor_add(out=acc[1][:, 1, :], in0=acc[1][:, 1, :], in1=last)
        nc.scalar.activation(out=rfac[:], in_=small[:, 0:NF], func=ACT.Abs_reciprocal_sqrt,
                             scale=small[:, NF + 1 : NF + 2])

        col_ps = bank()
        column_sum(col_ps, acc[1][:, 0, :], True, False)
        held.append(gradient(2, 0))
        column_sum(col_ps, acc[1][:, 1, :], False, True)
        column_factor(1, col_ps)

        rows = {}

        def update(f, h, ps):
            if h == 0:
                rows[f] = outs.tile([P, N], F32, name="row")
            nc.vector.scalar_tensor_tensor(out=rows[f][:, h * HALF : (h + 1) * HALF], in0=ps[:], scalar=rfac[:, f : f + 1],
                                           in1=cfac[h][:], op0=ALU.mult, op1=ALU.mult)

        def store(f, cols):
            nc.sync.dma_start(out=out[f * P : (f + 1) * P, cols], in_=rows[f][:, cols])

        halves = (slice(0, HALF), slice(HALF, N))
        for h in range(2):
            for f in range(4):
                update(f, h, held[f] if h == 0 and f < len(held) else gradient(f, h))
                store(f, halves[h])
        for f in range(4, NF):
            for h in range(2):
                update(f, h, gradient(f, h))
                if f == NF - 1:
                    store(f, halves[h])
            if f < NF - 1:
                store(f, slice(0, N))
